import numpy as np
import ml_dtypes


def mxq(x, axis, fmt="e4m3"):
    dtype, down = {"e4m3": (ml_dtypes.float8_e4m3fn, 7), "e5m2": (ml_dtypes.float8_e5m2, 14)}[fmt]
    v = np.moveaxis(np.asarray(x, np.float32).astype(ml_dtypes.bfloat16).astype(np.float64), axis, -1)
    blocks = v.reshape(v.shape[:-1] + (-1, 32))
    amax = np.abs(blocks).max(-1, keepdims=True)
    byte = np.maximum(np.where(amax > 0, np.frexp(amax)[1] - 1 + 127, 0) - down, 1)
    scale = np.exp2(byte - 127.0)
    codes = (blocks / scale).astype(np.float32).astype(dtype).astype(np.float64)
    return np.moveaxis((codes * scale).reshape(v.shape), -1, axis)


WIDE = False


def mx_kscale(k):
    if not WIDE:
        return np.ones(k)
    levels = np.array([10, -10, 5, -5, 0])
    if k % 512:
        return np.exp2(np.random.permutation(np.resize(levels, k // 32))).repeat(32)
    a = np.empty((k // 512, 16))
    for p in range(k // 512):
        a[p, :8] = np.random.permutation(np.resize(levels, 8))
        for g in range(8):
            far = levels[np.abs(levels - a[p, g]) >= 10]
            a[p, g + 8] = far[np.random.randint(len(far))]
    return np.exp2(a.ravel()).repeat(32)


def f64(x):
    return np.asarray(x).astype(np.float64)


def striped(idx):
    return np.tile(idx.reshape(-1, 16).T, (8, 1)).astype(np.uint16)


def unstriped(offs):
    return offs[:16].T.reshape(-1).astype(np.int64)


E2M1 = np.array([0.0, 0.5, 1.0, 1.5, 2.0, 3.0, 4.0, 6.0, -0.0, -0.5, -1.0, -1.5, -2.0, -3.0, -4.0, -6.0])


def pack_weight(w, fmt):
    k, n = w.shape
    w = f64(np.asarray(w, np.float32).astype(ml_dtypes.bfloat16)).reshape(k // 32, 32, n)
    amax = np.abs(w).max(1)
    if fmt == "e4m3":
        byte = np.frexp(amax)[1] - 1 + 127 - 7
    else:
        mant, ex = np.frexp(amax / 6.0)
        byte = np.where(mant > 0.5, ex, ex - 1) + 127
    byte = np.clip(np.where(amax > 0, byte, 1), 1, 254)
    scaled = (w * np.exp2(127.0 - byte)[:, None, :]).reshape(k, n).astype(np.float32)
    by_word = np.ascontiguousarray(scaled.reshape(k // 512, 128, 4, n).transpose(0, 1, 3, 2))
    if fmt == "e4m3":
        words = by_word.astype(ml_dtypes.float8_e4m3fn).view(np.uint8)
    else:
        c = by_word.astype(ml_dtypes.float4_e2m1fn).view(np.uint8) & 0xF
        words = (c[..., 0::2] | (c[..., 1::2] << 4)).reshape(k // 512, 128, 2 * n)
    return np.ascontiguousarray(words), np.ascontiguousarray(byte.astype(np.uint8).reshape(k // 512, 16, n))


def unpack_weight(words, scales, fmt):
    g, _, n = scales.shape
    words = np.ascontiguousarray(words).reshape(g, 128, n, -1)
    if fmt == "e4m3":
        vals = words.view(ml_dtypes.float8_e4m3fn).astype(np.float64)
    else:
        nib = np.empty((g, 128, n, 4), np.uint8)
        nib[..., 0::2] = words & 0xF
        nib[..., 1::2] = words >> 4
        vals = E2M1[nib]
    vals = vals * np.repeat(np.exp2(scales.astype(np.float64) - 127.0), 8, axis=1)[..., None]
    return vals.transpose(0, 1, 3, 2).reshape(g * 512, n)


K, T, E, B, H, N = 512, 1024, 6, 4, 512, 512


def setup_inputs():
    n = np.random.standard_normal
    s = mx_kscale(K)
    u = mx_kscale(H)
    slot_token = np.random.permutation(T)[:128 * B]
    block = np.sort(np.random.randint(E, size=B))
    x = pack_weight(n((K, T)) * s[:, None], "e4m3")
    wa = pack_weight(n((K, E * H)) / np.sqrt(K) / s[:, None] * np.tile(u, E), "e4m3")
    wb = pack_weight(n((H, E * N)) / np.sqrt(H) / u[:, None], "e4m3")
    return {
        "x_words": x[0],
        "x_scales": x[1],
        "w": (n((K, N)) / np.sqrt(K) / s[:, None]).astype(np.float32),
        "wa_words": wa[0],
        "wa_scales": wa[1],
        "wb_words": wb[0],
        "wb_scales": wb[1],
        "gate": (np.tile(np.random.uniform(0.2, 1.0, 128 * B), (128, 1))).astype(np.float32),
        "offs": striped(slot_token),
        "offs2": striped((block[:, None] * H + np.arange(H)).reshape(-1)),
        "offs3": striped((block[:, None] * N + np.arange(N)).reshape(-1)),
    }


def reference(x_words, x_scales, w, wa_words, wa_scales, wb_words, wb_scales, gate, offs, offs2, offs3):
    wq = mxq(f64(w), 0, "e4m3")
    idx, idx2, idx3 = unstriped(offs), unstriped(offs2), unstriped(offs3)
    x = unpack_weight(x_words, x_scales, "e4m3")
    out = wq.T @ x
    wa = unpack_weight(wa_words, wa_scales, "e4m3")[:, idx2]
    wb = unpack_weight(wb_words, wb_scales, "e4m3")[:, idx3]
    xq = x[:, idx]
    h = np.concatenate([wa[:, m * H:(m + 1) * H].T @ xq[:, 128 * m:128 * m + 128] for m in range(B)], axis=1)
    hq = mxq(h, 0, "e4m3")
    y = np.concatenate([wb[:, m * N:(m + 1) * N].T @ hq[:, 128 * m:128 * m + 128] for m in range(B)], axis=1)
    out[:, idx] += f64(gate[:1]) * y
    return out

@@ -1,0 +1,208 @@
+from contextlib import ExitStack
+
+import concourse.mybir as mybir
+from concourse.masks import make_identity
+
+K, T, E, B, H, N = 512, 1024, 6, 4, 512, 512
+P = 128
+SLOTS = P * B
+FLOPS = 2 * K * N * T + 2 * K * H * SLOTS + 2 * H * N * SLOTS
+
+F32 = mybir.dt.float32
+BF16 = mybir.dt.bfloat16
+I32 = mybir.dt.int32
+U32 = mybir.dt.uint32
+U16 = mybir.dt.uint16
+U8 = mybir.dt.uint8
+FP8X4 = mybir.dt.float8_e4m3fn_x4
+COPY = mybir.ActivationFunctionType.Copy
+
+X_ROW, WA_ROW, WB_ROW = 0, 4, 8
+
+
+def tile_moe_dyl_none_kernel(
+    tc, x_words, x_scales, w, wa_words, wa_scales, wb_words, wb_scales, gate, offs, offs2, offs3, out
+):
+    nc = tc.nc
+    with ExitStack() as ctx:
+        lists = ctx.enter_context(tc.tile_pool(name="lists", bufs=1))
+        sb = ctx.enter_context(tc.tile_pool(name="sb", bufs=1))
+        ps = ctx.enter_context(tc.psum_pool(name="ps", bufs=1))
+
+        def tile(name, shape, dtype):
+            return sb.tile(shape, dtype, name=name, align_bytes=64)
+
+        tok_list = lists.tile([P, SLOTS // 16], U16, name="tok_list")
+        wa_list = lists.tile([P, B * H // 16], U16, name="wa_list")
+        wb_list = lists.tile([P, B * N // 16], U16, name="wb_list")
+
+        x_w = tile("x_w", [P, T], U32)
+        x_s = tile("x_s", [P, T], U8)
+        wa_w = tile("wa_w", [P, E * H], U32)
+        wa_s = tile("wa_s", [P, E * H], U8)
+        wb_w = tile("wb_w", [P, E * N], U32)
+        wb_s = tile("wb_s", [P, E * N], U8)
+        xg_w = tile("xg_w", [P, SLOTS], U32)
+        xg_s = tile("xg_s", [P, SLOTS], U8)
+        wag_w = tile("wag_w", [P, B * H], U32)
+        wag_s = tile("wag_s", [P, B * H], U8)
+        wbg_w = tile("wbg_w", [P, B * N], U32)
+        wbg_s = tile("wbg_s", [P, B * N], U8)
+        w_raw = [tile("w_raw%d" % u, [P, 4, N // 2], F32) for u in range(2)]
+        w_bf = [tile("w_bf%d" % u, [P, N // 2, 4], BF16) for u in range(2)]
+        wq_w = tile("wq_w", [P, N], U32)
+        wq_s = tile("wq_s", [P, N], U8)
+        hq_w = tile("hq_w", [P, SLOTS], U32)
+        hq_s = tile("hq_s", [P, SLOTS], U8)
+        gate_rows = tile("gate_rows", [P, P], F32)
+        gate_col = tile("gate_col", [P, B], F32)
+        ident = tile("ident", [P, P], F32)
+        h_rows = [tile("h_rows%d" % m, [P, H], BF16) for m in range(B)]
+        h_bf = [tile("h_bf%d" % m, [P, P, 4], BF16) for m in range(B)]
+        base_rows = [tile("base_rows%d" % m, [P, N], F32) for m in range(B)]
+        gy_rows = [tile("gy_rows%d" % m, [P, N], F32) for m in range(B)]
+        slot_out = [[tile("slot_out%d%d" % (u, v), [P, 2, 2 * P], F32) for v in range(2)] for u in range(2)]
+        res = [tile("res%d" % c, [P, T], F32) for c in range(N // P)]
+        bank = [ps.tile([P, 512], F32, name="bank%d" % b) for b in range(8)]
+
+        def load_words(dst, src):
+            nc.sync.dma_start(out=dst[:].bitcast(I32), in_=src[0].rearrange("p c d -> p (c d)").bitcast(I32))
+
+        def load_scales(queue, plane, src, row):
+            for r in range(4):
+                queue.dma_start(out=plane[row + r : P : 32, :].bitcast(I32), in_=src[0][r:16:4, :].bitcast(I32))
+
+        def gather(dst, window, offsets, a, b):
+            nc.vector.tensor_copy(dst[:, a:b], window[:].indirect(offsets[:, a // 16 : b // 16]))
+
+        def mx(dst, lw, ls, lrow, lcols, rw, rs, rrow, rcols):
+            nc.tensor.matmul_mx(
+                out=dst, lhsT=lw[:, lcols].bitcast(FP8X4), lhsT_scale=ls[lrow:P, lcols],
+                rhs=rw[:, rcols].bitcast(FP8X4), rhs_scale=rs[rrow:P, rcols], start=True, stop=True,
+            )
+
+        def cols(i, width):
+            return slice(i * width, (i + 1) * width)
+
+        nc.vector.memset(wa_s[:].bitcast(I32), 0)
+        nc.vector.memset(x_s[:].bitcast(I32), 0)
+        nc.gpsimd.memset(wb_s[:].bitcast(I32), 0)
+
+        nc.sync.dma_start(wa_list[:], offs2)
+        nc.sync.dma_start(tok_list[:], offs)
+        nc.sync.dma_start(wb_list[:], offs3)
+        load_scales(nc.scalar, wa_s, wa_scales, WA_ROW)
+        for u in range(2):
+            nc.sync.dma_start(out=w_raw[u][:], in_=w[:, cols(u, N // 2)].rearrange("(p j) n -> p j n", j=4))
+        load_words(x_w, x_words)
+        load_words(wa_w, wa_words)
+        load_scales(nc.scalar, x_s, x_scales, X_ROW)
+        load_scales(nc.sync, wb_s, wb_scales, WB_ROW)
+        load_words(wb_w, wb_words)
+        nc.sync.dma_start(out=gate_rows[:], in_=gate[0:32, :].rearrange("r (m u) -> (r m) u", u=P))
+        make_identity(nc, ident[:])
+
+        def round_w(u):
+            nc.scalar.activation(
+                out=w_bf[u][:].rearrange("p (c i) j -> p c j i", i=4),
+                in_=w_raw[u][:].rearrange("p j (c i) -> p c j i", i=4), func=COPY)
+
+        def quant_w(u):
+            c = cols(u, N // 2)
+            nc.vector.quantize_mx(out=wq_w[:, c].bitcast(FP8X4), scales=wq_s[:, c], in_=w_bf[u][:].rearrange("p n j -> p (n j)"))
+
+        def base(c):
+            for t in range(2):
+                b = bank[(2 * c + t) % 4]
+                mx(b[:], wq_w, wq_s, 0, cols(c, P), x_w, x_s, X_ROW, cols(t, 512))
+                nc.scalar.copy(out=res[c][:, cols(t, 512)], in_=b[:])
+
+        def first(m, b):
+            mx(b[:], xg_w, xg_s, X_ROW, cols(m, P), wag_w, wag_s, WA_ROW, cols(m, H))
+            nc.scalar.copy(
+                out=h_rows[m][:].rearrange("s (u p e) -> s u p e", u=2, e=2),
+                in_=b[:].rearrange("s (p u e) -> s u p e", u=2, e=2))
+
+        def turn_h(m, b):
+            pairs = h_rows[m][:].bitcast(F32)
+            for u in range(2):
+                nc.tensor.transpose(b[:, cols(u, P)], pairs[:, cols(u, P)], ident[:])
+            nc.scalar.copy(
+                out=h_bf[m][:].rearrange("p s j -> p (s j)").bitcast(F32).rearrange("p (s u) -> p s u", u=2),
+                in_=b[:, 0 : 2 * P].rearrange("p (u s) -> p s u", u=2))
+
+        def quant_h(m):
+            c = cols(m, P)
+            nc.vector.quantize_mx(out=hq_w[:, c].bitcast(FP8X4), scales=hq_s[:, c], in_=h_bf[m][:].rearrange("p s j -> p (s j)"))
+
+        def slot_base(m, b):
+            mx(b[:], xg_w, xg_s, X_ROW, cols(m, P), wq_w, wq_s, 0, cols(0, N))
+            nc.scalar.copy(out=base_rows[m][:], in_=b[:])
+
+        def second(m, b):
+            mx(b[:], hq_w, hq_s, 0, cols(m, P), wbg_w, wbg_s, WB_ROW, cols(m, N))
+            nc.scalar.activation(out=gy_rows[m][:], in_=b[:], func=COPY, scale=gate_col[:, m : m + 1])
+
+        def combine(u, v, b):
+            for cc in range(2):
+                for mm in range(2):
+                    region = b[:, cols(2 * cc + mm, P)]
+                    m, c = 2 * u + mm, cols(2 * v + cc, P)
+                    nc.tensor.matmul(region, base_rows[m][:, c], ident[:], start=True, stop=False, is_transpose=True)
+                    nc.tensor.matmul(region, gy_rows[m][:, c], ident[:], start=False, stop=True, is_transpose=True)
+            nc.scalar.copy(out=slot_out[u][v][:].rearrange("p a b -> p (a b)"), in_=b[:])
+
+        def scatter(u, c):
+            nc.vector.tensor_copy(res[c][:].indirect(tok_list[:, cols(u, 16)]), slot_out[u][c // 2][:, c % 2, :])
+
+        round_w(0)
+        round_w(1)
+        gather(wag_s, wa_s, wa_list, 0, 1024)
+        gather(wag_s, wa_s, wa_list, 1024, 2048)
+        quant_w(0)
+        quant_w(1)
+        for c in range(4):
+            base(c)
+        gather(xg_w, x_w, tok_list, 0, SLOTS)
+        gather(xg_s, x_s, tok_list, 0, SLOTS)
+        for m in range(B):
+            gather(wag_w, wa_w, wa_list, m * H, (m + 1) * H)
+        gather(wbg_s, wb_s, wb_list, 0, 1024)
+        gather(wbg_s, wb_s, wb_list, 1024, 2048)
+        nc.tensor.transpose(bank[7][:, 0:P], gate_rows[:], ident[:])
+        nc.scalar.copy(out=gate_col[:], in_=bank[7][:, 0:B])
+        first(0, bank[4])
+        first(1, bank[5])
+        turn_h(0, bank[6])
+        turn_h(1, bank[7])
+        slot_base(0, bank[0])
+        slot_base(1, bank[1])
+        gather(wbg_w, wb_w, wb_list, 0, N)
+        quant_h(0)
+        gather(wbg_w, wb_w, wb_list, N, 2 * N)
+        quant_h(1)
+        second(0, bank[2])
+        second(1, bank[3])
+        gather(wbg_w, wb_w, wb_list, 2 * N, 3 * N)
+        gather(wbg_w, wb_w, wb_list, 3 * N, 4 * N)
+        combine(0, 0, bank[0])
+        first(2, bank[3])
+        first(3, bank[2])
+        combine(0, 1, bank[1])
+        scatter(0, 0)
+        turn_h(2, bank[6])
+        turn_h(3, bank[7])
+        slot_base(2, bank[4])
+        slot_base(3, bank[5])
+        scatter(0, 1)
+        quant_h(2)
+        quant_h(3)
+        second(2, bank[0])
+        second(3, bank[1])
+        scatter(0, 2)
+        scatter(0, 3)
+        combine(1, 0, bank[2])
+        combine(1, 1, bank[3])
+        for c in range(4):
+            scatter(1, c)
+            nc.sync.dma_start(out=out[cols(c, P), :], in_=res[c][:])

@@ -46,8 +46,8 @@ def tile_moe_dyl_none_kernel(
         xg_s = tile("xg_s", [P, SLOTS], U8)
         wag_w = tile("wag_w", [P, B * H], U32)
         wag_s = tile("wag_s", [P, B * H], U8)
-        wbg_w = tile("wbg_w", [P, B * N], U32)
-        wbg_s = tile("wbg_s", [P, B * N], U8)
+        wbg_w = tile("wbg_w", [P, 2 * N], U32)
+        wbg_s = tile("wbg_s", [P, 2 * N], U8)
         w_raw = [tile("w_raw%d" % u, [P, 4, N // 2], F32) for u in range(2)]
         w_bf = [tile("w_bf%d" % u, [P, N // 2, 4], BF16) for u in range(2)]
         wq_w = tile("wq_w", [P, N], U32)
@@ -61,7 +61,7 @@ def tile_moe_dyl_none_kernel(
         h_bf = [tile("h_bf%d" % m, [P, P, 4], BF16) for m in range(B)]
         base_rows = [tile("base_rows%d" % m, [P, N], F32) for m in range(B)]
         gy_rows = [tile("gy_rows%d" % m, [P, N], F32) for m in range(B)]
-        slot_out = [[tile("slot_out%d%d" % (u, v), [P, 2, 2 * P], F32) for v in range(2)] for u in range(2)]
+        slot_out = [[tile("slot_out%d%d" % (u, c), [P, 2 * P], F32) for c in range(4)] for u in range(2)]
         res = [tile("res%d" % c, [P, T], F32) for c in range(N // P)]
         bank = [ps.tile([P, 512], F32, name="bank%d" % b) for b in range(8)]
 
@@ -72,8 +72,9 @@ def tile_moe_dyl_none_kernel(
             for r in range(4):
                 queue.dma_start(out=plane[row + r : P : 32, :].bitcast(I32), in_=src[0][r:16:4, :].bitcast(I32))
 
-        def gather(dst, window, offsets, a, b):
-            nc.vector.tensor_copy(dst[:, a:b], window[:].indirect(offsets[:, a // 16 : b // 16]))
+        def gather(dst, window, offsets, a, b, at=None):
+            at = a if at is None else at
+            nc.vector.tensor_copy(dst[:, at : at + b - a], window[:].indirect(offsets[:, a // 16 : b // 16]))
 
         def mx(dst, lw, ls, lrow, lcols, rw, rs, rrow, rcols):
             nc.tensor.matmul_mx(
@@ -85,21 +86,21 @@ def tile_moe_dyl_none_kernel(
             return slice(i * width, (i + 1) * width)
 
         nc.vector.memset(wa_s[:].bitcast(I32), 0)
-        nc.vector.memset(x_s[:].bitcast(I32), 0)
-        nc.gpsimd.memset(wb_s[:].bitcast(I32), 0)
+        nc.gpsimd.memset(x_s[:].bitcast(I32), 0)
+        nc.vector.memset(wb_s[:].bitcast(I32), 0)
 
-        nc.sync.dma_start(wa_list[:], offs2)
         nc.sync.dma_start(tok_list[:], offs)
-        nc.sync.dma_start(wb_list[:], offs3)
+        load_words(x_w, x_words)
+        nc.sync.dma_start(wa_list[:], offs2)
         load_scales(nc.scalar, wa_s, wa_scales, WA_ROW)
         for u in range(2):
             nc.sync.dma_start(out=w_raw[u][:], in_=w[:, cols(u, N // 2)].rearrange("(p j) n -> p j n", j=4))
-        load_words(x_w, x_words)
+        load_scales(nc.sync, x_s, x_scales, X_ROW)
+        nc.sync.dma_start(out=gate_rows[:], in_=gate[0:32, :].rearrange("r (m u) -> (r m) u", u=P))
         load_words(wa_w, wa_words)
-        load_scales(nc.scalar, x_s, x_scales, X_ROW)
+        nc.sync.dma_start(wb_list[:], offs3)
         load_scales(nc.sync, wb_s, wb_scales, WB_ROW)
         load_words(wb_w, wb_words)
-        nc.sync.dma_start(out=gate_rows[:], in_=gate[0:32, :].rearrange("r (m u) -> (r m) u", u=P))
         make_identity(nc, ident[:])
 
         def round_w(u):
@@ -140,69 +141,63 @@ def tile_moe_dyl_none_kernel(
             nc.scalar.copy(out=base_rows[m][:], in_=b[:])
 
         def second(m, b):
-            mx(b[:], hq_w, hq_s, 0, cols(m, P), wbg_w, wbg_s, WB_ROW, cols(m, N))
+            mx(b[:], hq_w, hq_s, 0, cols(m, P), wbg_w, wbg_s, WB_ROW, cols(m % 2, N))
             nc.scalar.activation(out=gy_rows[m][:], in_=b[:], func=COPY, scale=gate_col[:, m : m + 1])
 
-        def combine(u, v, b):
-            for cc in range(2):
-                for mm in range(2):
-                    region = b[:, cols(2 * cc + mm, P)]
-                    m, c = 2 * u + mm, cols(2 * v + cc, P)
-                    nc.tensor.matmul(region, base_rows[m][:, c], ident[:], start=True, stop=False, is_transpose=True)
-                    nc.tensor.matmul(region, gy_rows[m][:, c], ident[:], start=False, stop=True, is_transpose=True)
-            nc.scalar.copy(out=slot_out[u][v][:].rearrange("p a b -> p (a b)"), in_=b[:])
+        def combine(u, c, b):
+            for mm in range(2):
+                region = b[:, cols(mm, P)]
+                m = 2 * u + mm
+                nc.tensor.matmul(region, base_rows[m][:, cols(c, P)], ident[:], start=True, stop=False, is_transpose=True)
+                nc.tensor.matmul(region, gy_rows[m][:, cols(c, P)], ident[:], start=False, stop=True, is_transpose=True)
+            nc.scalar.copy(out=slot_out[u][c][:], in_=b[:, 0 : 2 * P])
 
         def scatter(u, c):
-            nc.vector.tensor_copy(res[c][:].indirect(tok_list[:, cols(u, 16)]), slot_out[u][c // 2][:, c % 2, :])
+            nc.vector.tensor_copy(res[c][:].indirect(tok_list[:, cols(u, 16)]), slot_out[u][c][:])
 
         round_w(0)
         round_w(1)
+        gather(xg_w, x_w, tok_list, 0, SLOTS)
         gather(wag_s, wa_s, wa_list, 0, 1024)
-        gather(wag_s, wa_s, wa_list, 1024, 2048)
         quant_w(0)
+        gather(wag_s, wa_s, wa_list, 1024, 2048)
         quant_w(1)
+        nc.tensor.transpose(bank[7][:, 0:P], gate_rows[:], ident[:])
+        nc.scalar.copy(out=gate_col[:], in_=bank[7][:, 0:B])
         for c in range(4):
             base(c)
-        gather(xg_w, x_w, tok_list, 0, SLOTS)
         gather(xg_s, x_s, tok_list, 0, SLOTS)
         for m in range(B):
             gather(wag_w, wa_w, wa_list, m * H, (m + 1) * H)
         gather(wbg_s, wb_s, wb_list, 0, 1024)
-        gather(wbg_s, wb_s, wb_list, 1024, 2048)
-        nc.tensor.transpose(bank[7][:, 0:P], gate_rows[:], ident[:])
-        nc.scalar.copy(out=gate_col[:], in_=bank[7][:, 0:B])
         first(0, bank[4])
         first(1, bank[5])
         turn_h(0, bank[6])
         turn_h(1, bank[7])
         slot_base(0, bank[0])
         slot_base(1, bank[1])
-        gather(wbg_w, wb_w, wb_list, 0, N)
-        quant_h(0)
-        gather(wbg_w, wb_w, wb_list, N, 2 * N)
-        quant_h(1)
-        second(0, bank[2])
-        second(1, bank[3])
-        gather(wbg_w, wb_w, wb_list, 2 * N, 3 * N)
-        gather(wbg_w, wb_w, wb_list, 3 * N, 4 * N)
-        combine(0, 0, bank[0])
-        first(2, bank[3])
-        first(3, bank[2])
-        combine(0, 1, bank[1])
-        scatter(0, 0)
+        first(2, bank[4])
+        first(3, bank[5])
         turn_h(2, bank[6])
         turn_h(3, bank[7])
-        slot_base(2, bank[4])
-        slot_base(3, bank[5])
-        scatter(0, 1)
-        quant_h(2)
-        quant_h(3)
-        second(2, bank[0])
-        second(3, bank[1])
-        scatter(0, 2)
-        scatter(0, 3)
-        combine(1, 0, bank[2])
-        combine(1, 1, bank[3])
+        slot_base(2, bank[2])
+        slot_base(3, bank[3])
+        for m in range(2):
+            gather(wbg_w, wb_w, wb_list, m * N, (m + 1) * N)
+            quant_h(m)
+            second(m, bank[m])
+        for m in range(2, 4):
+            gather(wbg_s, wb_s, wb_list, m * N, (m + 1) * N, at=(m % 2) * N)
+            gather(wbg_w, wb_w, wb_list, m * N, (m + 1) * N, at=(m % 2) * N)
+        for c in range(4):
+            combine(0, c, bank[4 + c])
+        for m in range(2, 4):
+            quant_h(m)
+            second(m, bank[m])
+        for c in range(4):
+            scatter(0, c)
+        for c in range(4):
+            combine(1, c, bank[4 + c])
         for c in range(4):
             scatter(1, c)
             nc.sync.dma_start(out=out[cols(c, P), :], in_=res[c][:])

@@ -49,28 +49,28 @@ def tile_moe_dyl_none_kernel(
         wbg_w = tile("wbg_w", [P, 2 * N], U32)
         wbg_s = tile("wbg_s", [P, 2 * N], U8)
         w_raw = [tile("w_raw%d" % u, [P, 4, N // 2], F32) for u in range(2)]
-        w_bf = [tile("w_bf%d" % u, [P, N // 2, 4], BF16) for u in range(2)]
+        w_bf = tile("w_bf", [P, N, 4], BF16)
         wq_w = tile("wq_w", [P, N], U32)
         wq_s = tile("wq_s", [P, N], U8)
-        hq_w = tile("hq_w", [P, SLOTS], U32)
-        hq_s = tile("hq_s", [P, SLOTS], U8)
+        hq_w = tile("hq_w", [P, 2 * P], U32)
+        hq_s = tile("hq_s", [P, 2 * P], U8)
         gate_rows = tile("gate_rows", [P, P], F32)
         gate_col = tile("gate_col", [P, B], F32)
         ident = tile("ident", [P, P], F32)
         h_rows = [tile("h_rows%d" % m, [P, H], BF16) for m in range(B)]
-        h_bf = [tile("h_bf%d" % m, [P, P, 4], BF16) for m in range(B)]
+        h_bf = [tile("h_bf%d" % u, [P, 2 * P, 4], BF16) for u in range(2)]
         base_rows = [tile("base_rows%d" % m, [P, N], F32) for m in range(B)]
         gy_rows = [tile("gy_rows%d" % m, [P, N], F32) for m in range(B)]
-        slot_out = [[tile("slot_out%d%d" % (u, c), [P, 2 * P], F32) for c in range(4)] for u in range(2)]
+        slot_out = [tile("slot_out%d" % c, [P, SLOTS], F32) for c in range(4)]
         res = [tile("res%d" % c, [P, T], F32) for c in range(N // P)]
         bank = [ps.tile([P, 512], F32, name="bank%d" % b) for b in range(8)]
 
-        def load_words(dst, src):
-            nc.sync.dma_start(out=dst[:].bitcast(I32), in_=src[0].rearrange("p c d -> p (c d)").bitcast(I32))
+        def load_words(queue, dst, src):
+            queue.dma_start(out=dst[:].bitcast(I32), in_=src[0].rearrange("p c d -> p (c d)").bitcast(I32))
 
-        def load_scales(queue, plane, src, row):
+        def load_scales(queues, plane, src, row):
             for r in range(4):
-                queue.dma_start(out=plane[row + r : P : 32, :].bitcast(I32), in_=src[0][r:16:4, :].bitcast(I32))
+                queues[r % len(queues)].dma_start(out=plane[row + r : P : 32, :].bitcast(I32), in_=src[0][r:16:4, :].bitcast(I32))
 
         def gather(dst, window, offsets, a, b, at=None):
             at = a if at is None else at
@@ -85,36 +85,35 @@ def tile_moe_dyl_none_kernel(
         def cols(i, width):
             return slice(i * width, (i + 1) * width)
 
-        nc.vector.memset(wa_s[:].bitcast(I32), 0)
         nc.gpsimd.memset(x_s[:].bitcast(I32), 0)
-        nc.vector.memset(wb_s[:].bitcast(I32), 0)
+        nc.vector.memset(wa_s[:].bitcast(I32), 0)
+        nc.gpsimd.memset(wb_s[:].bitcast(I32), 0)
 
+        load_words(nc.scalar, x_w, x_words)
         nc.sync.dma_start(tok_list[:], offs)
-        load_words(x_w, x_words)
-        nc.sync.dma_start(wa_list[:], offs2)
-        load_scales(nc.scalar, wa_s, wa_scales, WA_ROW)
+        load_scales([nc.scalar, nc.sync], x_s, x_scales, X_ROW)
         for u in range(2):
             nc.sync.dma_start(out=w_raw[u][:], in_=w[:, cols(u, N // 2)].rearrange("(p j) n -> p j n", j=4))
-        load_scales(nc.sync, x_s, x_scales, X_ROW)
+        nc.sync.dma_start(wa_list[:], offs2)
+        load_scales([nc.sync], wa_s, wa_scales, WA_ROW)
         nc.sync.dma_start(out=gate_rows[:], in_=gate[0:32, :].rearrange("r (m u) -> (r m) u", u=P))
-        load_words(wa_w, wa_words)
+        load_words(nc.sync, wa_w, wa_words)
         nc.sync.dma_start(wb_list[:], offs3)
-        load_scales(nc.sync, wb_s, wb_scales, WB_ROW)
-        load_words(wb_w, wb_words)
+        load_scales([nc.sync], wb_s, wb_scales, WB_ROW)
+        load_words(nc.sync, wb_w, wb_words)
         make_identity(nc, ident[:])
 
         def round_w(u):
             nc.scalar.activation(
-                out=w_bf[u][:].rearrange("p (c i) j -> p c j i", i=4),
+                out=w_bf[:, cols(u, N // 2), :].rearrange("p (c i) j -> p c j i", i=4),
                 in_=w_raw[u][:].rearrange("p j (c i) -> p c j i", i=4), func=COPY)
 
-        def quant_w(u):
-            c = cols(u, N // 2)
-            nc.vector.quantize_mx(out=wq_w[:, c].bitcast(FP8X4), scales=wq_s[:, c], in_=w_bf[u][:].rearrange("p n j -> p (n j)"))
+        def quant_w():
+            nc.vector.quantize_mx(out=wq_w[:].bitcast(FP8X4), scales=wq_s[:], in_=w_bf[:].rearrange("p n j -> p (n j)"))
 
-        def base(c):
+        def base(c, first_bank):
             for t in range(2):
-                b = bank[(2 * c + t) % 4]
+                b = bank[first_bank + t]
                 mx(b[:], wq_w, wq_s, 0, cols(c, P), x_w, x_s, X_ROW, cols(t, 512))
                 nc.scalar.copy(out=res[c][:, cols(t, 512)], in_=b[:])
 
@@ -129,46 +128,48 @@ def tile_moe_dyl_none_kernel(
             for u in range(2):
                 nc.tensor.transpose(b[:, cols(u, P)], pairs[:, cols(u, P)], ident[:])
             nc.scalar.copy(
-                out=h_bf[m][:].rearrange("p s j -> p (s j)").bitcast(F32).rearrange("p (s u) -> p s u", u=2),
+                out=h_bf[m // 2][:, cols(m % 2, P), :].rearrange("p s j -> p (s j)").bitcast(F32).rearrange("p (s u) -> p s u", u=2),
                 in_=b[:, 0 : 2 * P].rearrange("p (u s) -> p s u", u=2))
 
         def quant_h(m):
-            c = cols(m, P)
-            nc.vector.quantize_mx(out=hq_w[:, c].bitcast(FP8X4), scales=hq_s[:, c], in_=h_bf[m][:].rearrange("p s j -> p (s j)"))
+            nc.vector.quantize_mx(out=hq_w[:].bitcast(FP8X4), scales=hq_s[:], in_=h_bf[m][:].rearrange("p s j -> p (s j)"))
 
         def slot_base(m, b):
             mx(b[:], xg_w, xg_s, X_ROW, cols(m, P), wq_w, wq_s, 0, cols(0, N))
             nc.scalar.copy(out=base_rows[m][:], in_=b[:])
 
         def second(m, b):
-            mx(b[:], hq_w, hq_s, 0, cols(m, P), wbg_w, wbg_s, WB_ROW, cols(m % 2, N))
+            mx(b[:], hq_w, hq_s, 0, cols(m % 2, P), wbg_w, wbg_s, WB_ROW, cols(m % 2, N))
             nc.scalar.activation(out=gy_rows[m][:], in_=b[:], func=COPY, scale=gate_col[:, m : m + 1])
 
-        def combine(u, c, b):
-            for mm in range(2):
+        def combine(c, blocks, b):
+            for mm, m in enumerate(blocks):
                 region = b[:, cols(mm, P)]
-                m = 2 * u + mm
                 nc.tensor.matmul(region, base_rows[m][:, cols(c, P)], ident[:], start=True, stop=False, is_transpose=True)
                 nc.tensor.matmul(region, gy_rows[m][:, cols(c, P)], ident[:], start=False, stop=True, is_transpose=True)
-            nc.scalar.copy(out=slot_out[u][c][:], in_=b[:, 0 : 2 * P])
+            nc.scalar.copy(out=slot_out[c][:, blocks[0] * P : (blocks[-1] + 1) * P], in_=b[:, 0 : len(blocks) * P])
 
-        def scatter(u, c):
-            nc.vector.tensor_copy(res[c][:].indirect(tok_list[:, cols(u, 16)]), slot_out[u][c][:])
+        def scatter(c, blocks):
+            a, b = blocks[0] * P, (blocks[-1] + 1) * P
+            nc.vector.tensor_copy(res[c][:].indirect(tok_list[:, a // 16 : b // 16]), slot_out[c][:, a:b])
+
+        def store(c):
+            nc.sync.dma_start(out=out[cols(c, P), :], in_=res[c][:])
 
         round_w(0)
         round_w(1)
         gather(xg_w, x_w, tok_list, 0, SLOTS)
+        gather(xg_s, x_s, tok_list, 0, SLOTS)
         gather(wag_s, wa_s, wa_list, 0, 1024)
-        quant_w(0)
+        quant_w()
         gather(wag_s, wa_s, wa_list, 1024, 2048)
-        quant_w(1)
         nc.tensor.transpose(bank[7][:, 0:P], gate_rows[:], ident[:])
         nc.scalar.copy(out=gate_col[:], in_=bank[7][:, 0:B])
-        for c in range(4):
-            base(c)
-        gather(xg_s, x_s, tok_list, 0, SLOTS)
-        for m in range(B):
-            gather(wag_w, wa_w, wa_list, m * H, (m + 1) * H)
+        base(0, 0)
+        base(1, 2)
+        gather(wag_w, wa_w, wa_list, 0, H)
+        gather(wag_w, wa_w, wa_list, H, 2 * H)
+        gather(wag_w, wa_w, wa_list, 1024, 2048)
         gather(wbg_s, wb_s, wb_list, 0, 1024)
         first(0, bank[4])
         first(1, bank[5])
@@ -176,28 +177,36 @@ def tile_moe_dyl_none_kernel(
         turn_h(1, bank[7])
         slot_base(0, bank[0])
         slot_base(1, bank[1])
-        first(2, bank[4])
-        first(3, bank[5])
-        turn_h(2, bank[6])
-        turn_h(3, bank[7])
-        slot_base(2, bank[2])
-        slot_base(3, bank[3])
+        first(2, bank[6])
+        first(3, bank[7])
+        turn_h(2, bank[4])
+        turn_h(3, bank[5])
+        quant_h(0)
         for m in range(2):
             gather(wbg_w, wb_w, wb_list, m * N, (m + 1) * N)
-            quant_h(m)
             second(m, bank[m])
+        gather(wbg_s, wb_s, wb_list, 2 * N, 3 * N, at=0)
+        gather(wbg_w, wb_w, wb_list, 2 * N, 3 * N, at=0)
+        quant_h(1)
+        gather(wbg_s, wb_s, wb_list, 3 * N, 4 * N, at=N)
+        gather(wbg_w, wb_w, wb_list, 3 * N, 4 * N, at=N)
+        combine(0, [0, 1], bank[2])
+        combine(1, [0, 1], bank[3])
+        slot_base(2, bank[0])
+        slot_base(3, bank[1])
         for m in range(2, 4):
-            gather(wbg_s, wb_s, wb_list, m * N, (m + 1) * N, at=(m % 2) * N)
-            gather(wbg_w, wb_w, wb_list, m * N, (m + 1) * N, at=(m % 2) * N)
-        for c in range(4):
-            combine(0, c, bank[4 + c])
-        for m in range(2, 4):
-            quant_h(m)
             second(m, bank[m])
-        for c in range(4):
-            scatter(0, c)
-        for c in range(4):
-            combine(1, c, bank[4 + c])
-        for c in range(4):
-            scatter(1, c)
-            nc.sync.dma_start(out=out[cols(c, P), :], in_=res[c][:])
+        scatter(0, [0, 1])
+        scatter(1, [0, 1])
+        combine(0, [2, 3], bank[6])
+        combine(1, [2, 3], bank[7])
+        base(2, 0)
+        combine(2, [0, 1, 2, 3], bank[4])
+        base(3, 0)
+        combine(3, [0, 1, 2, 3], bank[5])
+        for c in range(2):
+            scatter(c, [2, 3])
+            store(c)
+        for c in range(2, 4):
+            scatter(c, [0, 1, 2, 3])
+            store(c)

@@ -29,8 +29,8 @@ def tile_moe_dyl_none_kernel(
         sb = ctx.enter_context(tc.tile_pool(name="sb", bufs=1))
         ps = ctx.enter_context(tc.psum_pool(name="ps", bufs=1))
 
-        def tile(name, shape, dtype):
-            return sb.tile(shape, dtype, name=name, align_bytes=64)
+        def tile(name, shape, dtype, tag=""):
+            return sb.tile(shape, dtype, name=name, align_bytes=64, tag=tag)
 
         tok_list = lists.tile([P, SLOTS // 16], U16, name="tok_list")
         wa_list = lists.tile([P, B * H // 16], U16, name="wa_list")
@@ -38,7 +38,7 @@ def tile_moe_dyl_none_kernel(
 
         x_w = tile("x_w", [P, T], U32)
         x_s = tile("x_s", [P, T], U8)
-        wa_w = tile("wa_w", [P, E * H], U32)
+        wa_w = tile("wa_w", [P, E * H], U32, tag="wa_pool")
         wa_s = tile("wa_s", [P, E * H], U8)
         wb_w = tile("wb_w", [P, E * N], U32)
         wb_s = tile("wb_s", [P, E * N], U8)
@@ -47,7 +47,6 @@ def tile_moe_dyl_none_kernel(
         wag_w = tile("wag_w", [P, B * H], U32)
         wag_s = tile("wag_s", [P, B * H], U8)
         wbg_w = tile("wbg_w", [P, 2 * N], U32)
-        wbg_s = tile("wbg_s", [P, 2 * N], U8)
         w_raw = [tile("w_raw%d" % u, [P, 4, N // 2], F32) for u in range(2)]
         w_bf = tile("w_bf", [P, N, 4], BF16)
         wq_w = tile("wq_w", [P, N], U32)
@@ -59,7 +58,7 @@ def tile_moe_dyl_none_kernel(
         ident = tile("ident", [P, P], F32)
         h_rows = [tile("h_rows%d" % m, [P, H], BF16) for m in range(B)]
         h_bf = [tile("h_bf%d" % u, [P, 2 * P, 4], BF16) for u in range(2)]
-        base_rows = [tile("base_rows%d" % m, [P, N], F32) for m in range(B)]
+        base_rows = [[tile("base_rows%d%d" % (u, v), [P, 2, N // 2], F32) for v in range(2)] for u in range(2)]
         gy_rows = [tile("gy_rows%d" % m, [P, N], F32) for m in range(B)]
         slot_out = [tile("slot_out%d" % c, [P, SLOTS], F32) for c in range(4)]
         res = [tile("res%d" % c, [P, T], F32) for c in range(N // P)]
@@ -89,18 +88,21 @@ def tile_moe_dyl_none_kernel(
         nc.vector.memset(wa_s[:].bitcast(I32), 0)
         nc.gpsimd.memset(wb_s[:].bitcast(I32), 0)
 
+        def load_w(u):
+            nc.sync.dma_start(out=w_raw[u][:], in_=w[:, cols(u, N // 2)].rearrange("(p j) n -> p j n", j=4))
+
         load_words(nc.scalar, x_w, x_words)
         nc.sync.dma_start(tok_list[:], offs)
-        load_scales([nc.scalar, nc.sync], x_s, x_scales, X_ROW)
-        for u in range(2):
-            nc.sync.dma_start(out=w_raw[u][:], in_=w[:, cols(u, N // 2)].rearrange("(p j) n -> p j n", j=4))
         nc.sync.dma_start(wa_list[:], offs2)
+        load_scales([nc.scalar, nc.sync], x_s, x_scales, X_ROW)
+        load_w(0)
         load_scales([nc.sync], wa_s, wa_scales, WA_ROW)
-        nc.sync.dma_start(out=gate_rows[:], in_=gate[0:32, :].rearrange("r (m u) -> (r m) u", u=P))
         load_words(nc.sync, wa_w, wa_words)
+        nc.sync.dma_start(out=gate_rows[:], in_=gate[0:32, :].rearrange("r (m u) -> (r m) u", u=P))
         nc.sync.dma_start(wb_list[:], offs3)
         load_scales([nc.sync], wb_s, wb_scales, WB_ROW)
         load_words(nc.sync, wb_w, wb_words)
+        load_w(1)
         make_identity(nc, ident[:])
 
         def round_w(u):
@@ -108,8 +110,9 @@ def tile_moe_dyl_none_kernel(
                 out=w_bf[:, cols(u, N // 2), :].rearrange("p (c i) j -> p c j i", i=4),
                 in_=w_raw[u][:].rearrange("p j (c i) -> p c j i", i=4), func=COPY)
 
-        def quant_w():
-            nc.vector.quantize_mx(out=wq_w[:].bitcast(FP8X4), scales=wq_s[:], in_=w_bf[:].rearrange("p n j -> p (n j)"))
+        def quant_w(u):
+            c = cols(u, N // 2)
+            nc.vector.quantize_mx(out=wq_w[:, c].bitcast(FP8X4), scales=wq_s[:, c], in_=w_bf[:, c, :].rearrange("p n j -> p (n j)"))
 
         def base(c, first_bank):
             for t in range(2):
@@ -134,9 +137,10 @@ def tile_moe_dyl_none_kernel(
         def quant_h(m):
             nc.vector.quantize_mx(out=hq_w[:].bitcast(FP8X4), scales=hq_s[:], in_=h_bf[m][:].rearrange("p s j -> p (s j)"))
 
-        def slot_base(m, b):
-            mx(b[:], xg_w, xg_s, X_ROW, cols(m, P), wq_w, wq_s, 0, cols(0, N))
-            nc.scalar.copy(out=base_rows[m][:], in_=b[:])
+        def slot_base(u, v, b):
+            for mm in range(2):
+                mx(b[:, cols(mm, N // 2)], xg_w, xg_s, X_ROW, cols(2 * v + mm, P), wq_w, wq_s, 0, cols(u, N // 2))
+            nc.scalar.copy(out=base_rows[u][v][:].rearrange("s a n -> s (a n)"), in_=b[:])
 
         def second(m, b):
             mx(b[:], hq_w, hq_s, 0, cols(m % 2, P), wbg_w, wbg_s, WB_ROW, cols(m % 2, N))
@@ -145,7 +149,7 @@ def tile_moe_dyl_none_kernel(
         def combine(c, blocks, b):
             for mm, m in enumerate(blocks):
                 region = b[:, cols(mm, P)]
-                nc.tensor.matmul(region, base_rows[m][:, cols(c, P)], ident[:], start=True, stop=False, is_transpose=True)
+                nc.tensor.matmul(region, base_rows[c // 2][m // 2][:, m % 2, cols(c % 2, P)], ident[:], start=True, stop=False, is_transpose=True)
                 nc.tensor.matmul(region, gy_rows[m][:, cols(c, P)], ident[:], start=False, stop=True, is_transpose=True)
             nc.scalar.copy(out=slot_out[c][:, blocks[0] * P : (blocks[-1] + 1) * P], in_=b[:, 0 : len(blocks) * P])
 
@@ -157,30 +161,30 @@ def tile_moe_dyl_none_kernel(
             nc.sync.dma_start(out=out[cols(c, P), :], in_=res[c][:])
 
         round_w(0)
-        round_w(1)
         gather(xg_w, x_w, tok_list, 0, SLOTS)
         gather(xg_s, x_s, tok_list, 0, SLOTS)
+        quant_w(0)
         gather(wag_s, wa_s, wa_list, 0, 1024)
-        quant_w()
         gather(wag_s, wa_s, wa_list, 1024, 2048)
-        nc.tensor.transpose(bank[7][:, 0:P], gate_rows[:], ident[:])
-        nc.scalar.copy(out=gate_col[:], in_=bank[7][:, 0:B])
         base(0, 0)
         base(1, 2)
         gather(wag_w, wa_w, wa_list, 0, H)
         gather(wag_w, wa_w, wa_list, H, 2 * H)
         gather(wag_w, wa_w, wa_list, 1024, 2048)
+        wbg_s = tile("wbg_s", [P, 2 * N], U8, tag="wa_pool")
         gather(wbg_s, wb_s, wb_list, 0, 1024)
         first(0, bank[4])
         first(1, bank[5])
         turn_h(0, bank[6])
-        turn_h(1, bank[7])
-        slot_base(0, bank[0])
-        slot_base(1, bank[1])
+        turn_h(1, bank[3])
+        slot_base(0, 0, bank[0])
+        nc.tensor.transpose(bank[0][:, 0:P], gate_rows[:], ident[:])
+        nc.scalar.copy(out=gate_col[:], in_=bank[0][:, 0:B])
         first(2, bank[6])
-        first(3, bank[7])
+        first(3, bank[3])
         turn_h(2, bank[4])
         turn_h(3, bank[5])
+        slot_base(0, 1, bank[5])
         quant_h(0)
         for m in range(2):
             gather(wbg_w, wb_w, wb_list, m * N, (m + 1) * N)
@@ -191,19 +195,21 @@ def tile_moe_dyl_none_kernel(
         gather(wbg_s, wb_s, wb_list, 3 * N, 4 * N, at=N)
         gather(wbg_w, wb_w, wb_list, 3 * N, 4 * N, at=N)
         combine(0, [0, 1], bank[2])
-        combine(1, [0, 1], bank[3])
-        slot_base(2, bank[0])
-        slot_base(3, bank[1])
-        for m in range(2, 4):
-            second(m, bank[m])
+        combine(1, [0, 1], bank[7])
+        second(2, bank[2])
+        second(3, bank[7])
+        round_w(1)
         scatter(0, [0, 1])
         scatter(1, [0, 1])
+        quant_w(1)
         combine(0, [2, 3], bank[6])
-        combine(1, [2, 3], bank[7])
-        base(2, 0)
-        combine(2, [0, 1, 2, 3], bank[4])
-        base(3, 0)
-        combine(3, [0, 1, 2, 3], bank[5])
+        combine(1, [2, 3], bank[3])
+        slot_base(1, 0, bank[0])
+        slot_base(1, 1, bank[1])
+        base(2, 4)
+        combine(2, [0, 1, 2, 3], bank[0])
+        base(3, 4)
+        combine(3, [0, 1, 2, 3], bank[1])
         for c in range(2):
             scatter(c, [2, 3])
             store(c)

from contextlib import ExitStack

import concourse.mybir as mybir
from concourse.masks import make_identity

K, T, E, B, H, N = 512, 1024, 6, 4, 512, 512
P = 128
SLOTS = P * B
FLOPS = 2 * K * N * T + 2 * K * H * SLOTS + 2 * H * N * SLOTS

F32 = mybir.dt.float32
BF16 = mybir.dt.bfloat16
I32 = mybir.dt.int32
U32 = mybir.dt.uint32
U16 = mybir.dt.uint16
U8 = mybir.dt.uint8
FP8X4 = mybir.dt.float8_e4m3fn_x4
COPY = mybir.ActivationFunctionType.Copy

X_ROW, WA_ROW, WB_ROW = 0, 4, 8


def tile_moe_dyl_none_kernel(
    tc, x_words, x_scales, w, wa_words, wa_scales, wb_words, wb_scales, gate, offs, offs2, offs3, out
):
    nc = tc.nc
    with ExitStack() as ctx:
        lists = ctx.enter_context(tc.tile_pool(name="lists", bufs=1))
        sb = ctx.enter_context(tc.tile_pool(name="sb", bufs=1))
        ps = ctx.enter_context(tc.psum_pool(name="ps", bufs=1))

        def tile(name, shape, dtype, tag=""):
            return sb.tile(shape, dtype, name=name, align_bytes=64, tag=tag)

        tok_list = lists.tile([P, SLOTS // 16], U16, name="tok_list")
        wa_list = lists.tile([P, B * H // 16], U16, name="wa_list")
        wb_list = lists.tile([P, B * N // 16], U16, name="wb_list")

        x_w = tile("x_w", [P, T], U32)
        x_s = tile("x_s", [P, T], U8)
        wa_w = tile("wa_w", [P, E * H], U32, tag="wa_pool")
        wa_s = tile("wa_s", [P, E * H], U8)
        wb_w = tile("wb_w", [P, E * N], U32)
        wb_s = tile("wb_s", [P, E * N], U8)
        xg_w = tile("xg_w", [P, SLOTS], U32)
        xg_s = tile("xg_s", [P, SLOTS], U8)
        wag_w = tile("wag_w", [P, B * H], U32)
        wag_s = tile("wag_s", [P, B * H], U8)
        wbg_w = tile("wbg_w", [P, 2 * N], U32)
        w_raw = [tile("w_raw%d" % u, [P, 4, N // 2], F32) for u in range(2)]
        w_bf = tile("w_bf", [P, N, 4], BF16)
        wq_w = tile("wq_w", [P, N], U32)
        wq_s = tile("wq_s", [P, N], U8)
        hq_w = tile("hq_w", [P, 2 * P], U32)
        hq_s = tile("hq_s", [P, 2 * P], U8)
        gate_rows = tile("gate_rows", [P, P], F32)
        gate_col = tile("gate_col", [P, B], F32)
        ident = tile("ident", [P, P], F32)
        h_rows = [tile("h_rows%d" % m, [P, H], BF16) for m in range(B)]
        h_bf = [tile("h_bf%d" % u, [P, 2 * P, 4], BF16) for u in range(2)]
        base_rows = [[tile("base_rows%d%d" % (u, v), [P, 2, N // 2], F32) for v in range(2)] for u in range(2)]
        gy_rows = [tile("gy_rows%d" % m, [P, N], F32) for m in range(B)]
        slot_out = [tile("slot_out%d" % c, [P, SLOTS], F32) for c in range(4)]
        res = [tile("res%d" % c, [P, T], F32) for c in range(N // P)]
        bank = [ps.tile([P, 512], F32, name="bank%d" % b) for b in range(8)]

        def load_words(queue, dst, src):
            queue.dma_start(out=dst[:].bitcast(I32), in_=src[0].rearrange("p c d -> p (c d)").bitcast(I32))

        def load_scales(queues, plane, src, row):
            for r in range(4):
                queues[r % len(queues)].dma_start(out=plane[row + r : P : 32, :].bitcast(I32), in_=src[0][r:16:4, :].bitcast(I32))

        def gather(dst, window, offsets, a, b, at=None):
            at = a if at is None else at
            nc.vector.tensor_copy(dst[:, at : at + b - a], window[:].indirect(offsets[:, a // 16 : b // 16]))

        def mx(dst, lw, ls, lrow, lcols, rw, rs, rrow, rcols):
            nc.tensor.matmul_mx(
                out=dst, lhsT=lw[:, lcols].bitcast(FP8X4), lhsT_scale=ls[lrow:P, lcols],
                rhs=rw[:, rcols].bitcast(FP8X4), rhs_scale=rs[rrow:P, rcols], start=True, stop=True,
            )

        def cols(i, width):
            return slice(i * width, (i + 1) * width)

        nc.gpsimd.memset(x_s[:].bitcast(I32), 0)
        nc.vector.memset(wa_s[:].bitcast(I32), 0)
        nc.gpsimd.memset(wb_s[:].bitcast(I32), 0)

        def load_w(u):
            nc.sync.dma_start(out=w_raw[u][:], in_=w[:, cols(u, N // 2)].rearrange("(p j) n -> p j n", j=4))

        load_words(nc.scalar, x_w, x_words)
        nc.sync.dma_start(tok_list[:], offs)
        nc.sync.dma_start(wa_list[:], offs2)
        load_scales([nc.scalar, nc.sync], x_s, x_scales, X_ROW)
        load_w(0)
        load_scales([nc.sync], wa_s, wa_scales, WA_ROW)
        load_words(nc.sync, wa_w, wa_words)
        nc.sync.dma_start(out=gate_rows[:], in_=gate[0:32, :].rearrange("r (m u) -> (r m) u", u=P))
        nc.sync.dma_start(wb_list[:], offs3)
        load_scales([nc.sync], wb_s, wb_scales, WB_ROW)
        load_words(nc.sync, wb_w, wb_words)
        load_w(1)
        make_identity(nc, ident[:])

        def round_w(u):
            nc.scalar.activation(
                out=w_bf[:, cols(u, N // 2), :].rearrange("p (c i) j -> p c j i", i=4),
                in_=w_raw[u][:].rearrange("p j (c i) -> p c j i", i=4), func=COPY)

        def quant_w(u):
            c = cols(u, N // 2)
            nc.vector.quantize_mx(out=wq_w[:, c].bitcast(FP8X4), scales=wq_s[:, c], in_=w_bf[:, c, :].rearrange("p n j -> p (n j)"))

        def base(c, first_bank):
            for t in range(2):
                b = bank[first_bank + t]
                mx(b[:], wq_w, wq_s, 0, cols(c, P), x_w, x_s, X_ROW, cols(t, 512))
                nc.scalar.copy(out=res[c][:, cols(t, 512)], in_=b[:])

        def first(m, b):
            mx(b[:], xg_w, xg_s, X_ROW, cols(m, P), wag_w, wag_s, WA_ROW, cols(m, H))
            nc.scalar.copy(
                out=h_rows[m][:].rearrange("s (u p e) -> s u p e", u=2, e=2),
                in_=b[:].rearrange("s (p u e) -> s u p e", u=2, e=2))

        def turn_h(m, b):
            pairs = h_rows[m][:].bitcast(F32)
            for u in range(2):
                nc.tensor.transpose(b[:, cols(u, P)], pairs[:, cols(u, P)], ident[:])
            nc.scalar.copy(
                out=h_bf[m // 2][:, cols(m % 2, P), :].rearrange("p s j -> p (s j)").bitcast(F32).rearrange("p (s u) -> p s u", u=2),
                in_=b[:, 0 : 2 * P].rearrange("p (u s) -> p s u", u=2))

        def quant_h(m):
            nc.vector.quantize_mx(out=hq_w[:].bitcast(FP8X4), scales=hq_s[:], in_=h_bf[m][:].rearrange("p s j -> p (s j)"))

        def slot_base(u, v, b):
            for mm in range(2):
                mx(b[:, cols(mm, N // 2)], xg_w, xg_s, X_ROW, cols(2 * v + mm, P), wq_w, wq_s, 0, cols(u, N // 2))
            nc.scalar.copy(out=base_rows[u][v][:].rearrange("s a n -> s (a n)"), in_=b[:])

        def second(m, b):
            mx(b[:], hq_w, hq_s, 0, cols(m % 2, P), wbg_w, wbg_s, WB_ROW, cols(m % 2, N))
            nc.scalar.activation(out=gy_rows[m][:], in_=b[:], func=COPY, scale=gate_col[:, m : m + 1])

        def combine(c, blocks, b):
            for mm, m in enumerate(blocks):
                region = b[:, cols(mm, P)]
                nc.tensor.matmul(region, base_rows[c // 2][m // 2][:, m % 2, cols(c % 2, P)], ident[:], start=True, stop=False, is_transpose=True)
                nc.tensor.matmul(region, gy_rows[m][:, cols(c, P)], ident[:], start=False, stop=True, is_transpose=True)
            nc.scalar.copy(out=slot_out[c][:, blocks[0] * P : (blocks[-1] + 1) * P], in_=b[:, 0 : len(blocks) * P])

        def scatter(c, blocks):
            a, b = blocks[0] * P, (blocks[-1] + 1) * P
            nc.vector.tensor_copy(res[c][:].indirect(tok_list[:, a // 16 : b // 16]), slot_out[c][:, a:b])

        def store(c):
            nc.sync.dma_start(out=out[cols(c, P), :], in_=res[c][:])

        round_w(0)
        gather(xg_w, x_w, tok_list, 0, SLOTS)
        gather(xg_s, x_s, tok_list, 0, SLOTS)
        quant_w(0)
        gather(wag_s, wa_s, wa_list, 0, 1024)
        gather(wag_s, wa_s, wa_list, 1024, 2048)
        base(0, 0)
        base(1, 2)
        gather(wag_w, wa_w, wa_list, 0, H)
        gather(wag_w, wa_w, wa_list, H, 2 * H)
        gather(wag_w, wa_w, wa_list, 1024, 2048)
        wbg_s = tile("wbg_s", [P, 2 * N], U8, tag="wa_pool")
        gather(wbg_s, wb_s, wb_list, 0, 1024)
        first(0, bank[4])
        first(1, bank[5])
        turn_h(0, bank[6])
        turn_h(1, bank[3])
        slot_base(0, 0, bank[0])
        nc.tensor.transpose(bank[0][:, 0:P], gate_rows[:], ident[:])
        nc.scalar.copy(out=gate_col[:], in_=bank[0][:, 0:B])
        first(2, bank[6])
        first(3, bank[3])
        turn_h(2, bank[4])
        turn_h(3, bank[5])
        slot_base(0, 1, bank[5])
        quant_h(0)
        for m in range(2):
            gather(wbg_w, wb_w, wb_list, m * N, (m + 1) * N)
            second(m, bank[m])
        gather(wbg_s, wb_s, wb_list, 2 * N, 3 * N, at=0)
        gather(wbg_w, wb_w, wb_list, 2 * N, 3 * N, at=0)
        quant_h(1)
        gather(wbg_s, wb_s, wb_list, 3 * N, 4 * N, at=N)
        gather(wbg_w, wb_w, wb_list, 3 * N, 4 * N, at=N)
        combine(0, [0, 1], bank[2])
        combine(1, [0, 1], bank[7])
        second(2, bank[2])
        second(3, bank[7])
        round_w(1)
        scatter(0, [0, 1])
        scatter(1, [0, 1])
        quant_w(1)
        combine(0, [2, 3], bank[6])
        combine(1, [2, 3], bank[3])
        slot_base(1, 0, bank[0])
        slot_base(1, 1, bank[1])
        base(2, 4)
        combine(2, [0, 1, 2, 3], bank[0])
        base(3, 4)
        combine(3, [0, 1, 2, 3], bank[1])
        for c in range(2):
            scatter(c, [2, 3])
            store(c)
        for c in range(2, 4):
            scatter(c, [0, 1, 2, 3])
            store(c)
